import numpy as np
import ml_dtypes


def mxq(x, axis, fmt="e4m3"):
    dtype, down = {"e4m3": (ml_dtypes.float8_e4m3fn, 7), "e5m2": (ml_dtypes.float8_e5m2, 14)}[fmt]
    v = np.moveaxis(np.asarray(x, np.float32).astype(ml_dtypes.bfloat16).astype(np.float64), axis, -1)
    blocks = v.reshape(v.shape[:-1] + (-1, 32))
    amax = np.abs(blocks).max(-1, keepdims=True)
    byte = np.maximum(np.where(amax > 0, np.frexp(amax)[1] - 1 + 127, 0) - down, 1)
    scale = np.exp2(byte - 127.0)
    codes = (blocks / scale).astype(np.float32).astype(dtype).astype(np.float64)
    return np.moveaxis((codes * scale).reshape(v.shape), -1, axis)


WIDE = False


def mx_kscale(k):
    if not WIDE:
        return np.ones(k)
    levels = np.array([30, -30])
    if k % 512:
        return np.exp2(np.random.permutation(np.resize(levels, k // 32))).repeat(32)
    a = np.empty((k // 512, 16))
    for p in range(k // 512):
        a[p, :8] = np.random.permutation(np.resize(levels, 8))
        for g in range(8):
            far = levels[np.abs(levels - a[p, g]) >= 10]
            a[p, g + 8] = far[np.random.randint(len(far))]
    return np.exp2(a.ravel()).repeat(32)


def f64(x):
    return np.asarray(x).astype(np.float64)


def striped(idx):
    return np.tile(np.asarray(idx).reshape(-1, 16).T, (8, 1)).astype(np.uint16)


def unstriped(offs):
    return offs[:16].T.reshape(-1).astype(np.int64)


E2M1 = np.array([0.0, 0.5, 1.0, 1.5, 2.0, 3.0, 4.0, 6.0, -0.0, -0.5, -1.0, -1.5, -2.0, -3.0, -4.0, -6.0])


def pack_weight(w, fmt):
    k, n = w.shape
    w = f64(np.asarray(w, np.float32).astype(ml_dtypes.bfloat16)).reshape(k // 32, 32, n)
    amax = np.abs(w).max(1)
    if fmt in ("e4m3", "e5m2"):
        byte = np.frexp(amax)[1] - 1 + 127 - (7 if fmt == "e4m3" else 14)
    else:
        mant, ex = np.frexp(amax / 6.0)
        byte = np.where(mant > 0.5, ex, ex - 1) + 127
    byte = np.clip(np.where(amax > 0, byte, 1), 1, 254)
    scaled = (w * np.exp2(127.0 - byte)[:, None, :]).reshape(k, n).astype(np.float32)
    by_word = np.ascontiguousarray(scaled.reshape(k // 512, 128, 4, n).transpose(0, 1, 3, 2))
    if fmt in ("e4m3", "e5m2"):
        words = by_word.astype(ml_dtypes.float8_e4m3fn if fmt == "e4m3" else ml_dtypes.float8_e5m2).view(np.uint8)
    else:
        c = by_word.astype(ml_dtypes.float4_e2m1fn).view(np.uint8) & 0xF
        words = (c[..., 0::2] | (c[..., 1::2] << 4)).reshape(k // 512, 128, 2 * n)
    return np.ascontiguousarray(words), np.ascontiguousarray(byte.astype(np.uint8).reshape(k // 512, 16, n))


def unpack_weight(words, scales, fmt):
    g, _, n = scales.shape
    words = np.ascontiguousarray(words).reshape(g, 128, n, -1)
    if fmt in ("e4m3", "e5m2"):
        vals = words.view(ml_dtypes.float8_e4m3fn if fmt == "e4m3" else ml_dtypes.float8_e5m2).astype(np.float64)
    else:
        nib = np.empty((g, 128, n, 4), np.uint8)
        nib[..., 0::2] = words & 0xF
        nib[..., 1::2] = words >> 4
        vals = E2M1[nib]
    vals = vals * np.repeat(np.exp2(scales.astype(np.float64) - 127.0), 8, axis=1)[..., None]
    return vals.transpose(0, 1, 3, 2).reshape(g * 512, n)


K, J, N, R, T = 512, 512, 256, 256, 1024


def setup_inputs():
    n = np.random.standard_normal
    idx = np.random.permutation(T)[:J]
    idx2 = np.random.permutation(T)[:J]
    fj = mx_kscale(J)
    fk = mx_kscale(K)
    gjp = pack_weight(n((J, N)) * np.exp(0.5 * n((J, 1))) / fj[:, None], "e5m2")
    drp = pack_weight(n((K, R)) * 1 / np.sqrt(K) / fk[:, None], "e4m3")
    return {
        "xf": (n((K, T))).astype(np.float32),
        "ra": (np.random.uniform(0.5, 1.5, (1, J)) * fj).astype(np.float32),
        "gj_words": gjp[0],
        "gj_scales": gjp[1],
        "fkr": (np.random.uniform(0.5, 1.5, (1, K)) * fk).astype(np.float32),
        "dr_words": drp[0],
        "dr_scales": drp[1],
        "old": (1.0 * n((R, N))).astype(np.float32),
        "offs": striped(idx),
        "offs2": striped(idx2),
    }


def reference(xf, ra, gj_words, gj_scales, fkr, dr_words, dr_scales, old, offs, offs2):
    idx = unstriped(offs)
    idx2 = unstriped(offs2)
    gju = unpack_weight(gj_words, gj_scales, "e5m2")
    dru = unpack_weight(dr_words, dr_scales, "e4m3")
    us = (f64(xf)[:, idx] - f64(xf)[:, idx2]) * f64(ra)
    ut = us.T
    uj = ut * f64(fkr)
    ujq = mxq(uj, 0, "e4m3")
    w = ujq.T @ gju
    wq = mxq(w, 0, "e5m2")
    v2 = dru.T @ wq
    y = 0.05 * v2 + 0.5 * f64(old)
    return y

@@ -1,0 +1,168 @@
+from contextlib import ExitStack
+
+import concourse.mybir as mybir
+from concourse.masks import make_identity
+
+K, J, N, R, T = 512, 512, 256, 256, 1024
+FLOPS = 2 * J * K * N + 2 * K * R * N
+
+F32 = mybir.dt.float32
+BF16 = mybir.dt.bfloat16
+I32 = mybir.dt.int32
+U32 = mybir.dt.uint32
+U16 = mybir.dt.uint16
+U8 = mybir.dt.uint8
+E4M3 = mybir.dt.float8_e4m3fn_x4
+E5M2 = mybir.dt.float8_e5m2_x4
+MULT = mybir.AluOpType.mult
+ADD = mybir.AluOpType.add
+SUB = mybir.AluOpType.subtract
+COPY = mybir.ActivationFunctionType.Copy
+
+P = 128
+PACK = 4
+PER_COL = 16
+HALF = N // 2
+
+
+def tile_list_directions_gaps_stored_mixed_kernel(
+    tc, xf, ra, gj_words, gj_scales, fkr, dr_words, dr_scales, old, offs, offs2, out
+):
+    nc = tc.nc
+    with ExitStack() as ctx:
+        keep = ctx.enter_context(tc.tile_pool(name="keep", bufs=1))
+        psum = ctx.enter_context(tc.psum_pool(name="psum", bufs=1))
+
+        first = keep.tile([P, J // PER_COL], U16, name="first")
+        second = keep.tile([P, J // PER_COL], U16, name="second")
+        x_rows = xf.rearrange("(p t) c -> t p c", t=PACK)
+        x = [keep.tile([P, T], F32, name="x%d" % t) for t in range(PACK)]
+        nc.sync.dma_start(x[0][:], x_rows[0])
+        nc.sync.dma_start(second[:], offs2)
+        nc.sync.dma_start(first[:], offs)
+        for t in range(1, PACK):
+            nc.sync.dma_start(x[t][:], x_rows[t])
+
+        ra_cols = keep.tile([P, PACK], F32, name="ra_cols")
+        fk_cols = keep.tile([P, PACK], F32, name="fk_cols")
+        nc.scalar.dma_start(ra_cols[:], ra.rearrange("o (p t) -> (o p) t", t=PACK))
+        nc.scalar.dma_start(fk_cols[:], fkr.rearrange("o (p t) -> (o p) t", t=PACK))
+
+        ident = keep.tile([P, P], F32, name="ident")
+        make_identity(nc, ident[:])
+
+        def load_packed(words, scales, width, name):
+            codes = keep.tile([P, width], U32, name=name + "_codes", align_bytes=64)
+            plane = keep.tile([P, width], U8, name=name + "_plane", align_bytes=64)
+            nc.gpsimd.memset(plane[:].bitcast(I32), 0)
+            nc.sync.dma_start(codes[:].bitcast(I32), words[0].rearrange("p n t -> p (n t)").bitcast(I32))
+            for q in range(4):
+                nc.sync.dma_start(
+                    plane[32 * q : 32 * q + 4, :].bitcast(I32), scales[0, 4 * q : 4 * q + 4, :].bitcast(I32)
+                )
+            return codes, plane
+
+        gj_codes, gj_plane = load_packed(gj_words, gj_scales, N, "gj")
+        old_sb = keep.tile([P, 2, N], F32, name="old_sb")
+        nc.sync.dma_start(old_sb[:], old.rearrange("(a p) n -> p a n", p=P))
+        dr_codes, dr_plane = load_packed(dr_words, dr_scales, R, "dr")
+
+        ra_all = psum.tile([P, PACK, P], F32, name="ra_all")
+        for s in range(PACK):
+            nc.tensor.transpose(ra_all[:, s, :], ra_cols[:, s : s + 1].to_broadcast([P, P]), ident[:])
+        ra_by_j = ra_all[:].rearrange("m s q -> m q s")
+
+        b = [keep.tile([P, J], F32, name="b%d" % t, tag="b%d" % t) for t in range(PACK)]
+        d = [keep.tile([P, J], F32, name="d%d" % t) for t in range(PACK)]
+        u = [keep.tile([P, J], BF16, name="u%d" % t) for t in range(PACK)]
+        grouped = [keep.tile([P, J], BF16, name="grouped%d" % t, align_bytes=64) for t in range(PACK)]
+        u_codes = [keep.tile([P, P], U32, name="u_codes%d" % t, align_bytes=64) for t in range(PACK)]
+        u_plane = [keep.tile([P, P], U8, name="u_plane%d" % t, align_bytes=64) for t in range(PACK)]
+        w_bank = [psum.tile([P, PACK, HALF], F32, name="w_bank%d" % h) for h in range(2)]
+
+        def gather_second(t):
+            nc.scalar.activation(b[t][:], x[t][:].indirect(second[:]), COPY)
+
+        def difference(t):
+            nc.vector.tensor_tensor(d[t][:], x[t][:].indirect(first[:]), b[t][:], SUB)
+
+        def weigh(t):
+            nc.vector.scalar_tensor_tensor(
+                u[t][:].rearrange("p (q s) -> p q s", s=PACK),
+                d[t][:].rearrange("p (q s) -> p q s", s=PACK),
+                fk_cols[:, t : t + 1],
+                ra_by_j,
+                MULT,
+                MULT,
+            )
+
+        def turn(t):
+            words = u[t][:].bitcast(F32)
+            turned = psum.tile([P, 2, P], F32, name="turned%d" % t, tag="turned%d" % (t % 2))
+            for e in range(2):
+                nc.tensor.transpose(turned[:, e, :], words[:, e::2], ident[:])
+            nc.scalar.copy(
+                grouped[t][:].bitcast(F32).rearrange("p (m e) -> p m e", e=2),
+                turned[:].rearrange("p e m -> p m e"),
+            )
+
+        def first_product(t):
+            nc.vector.quantize_mx(out=u_codes[t][:].bitcast(E4M3), scales=u_plane[t][:], in_=grouped[t][:])
+            for h in range(2):
+                n_cols = slice(h * HALF, (h + 1) * HALF)
+                nc.tensor.matmul_mx(
+                    out=w_bank[h][:, t, :],
+                    lhsT=u_codes[t][:].bitcast(E4M3),
+                    lhsT_scale=u_plane[t][:],
+                    rhs=gj_codes[:, n_cols].bitcast(E5M2),
+                    rhs_scale=gj_plane[:, n_cols],
+                    start=True,
+                    stop=True,
+                )
+
+        gather_second(0)
+        difference(0)
+        for t in range(1, PACK):
+            gather_second(t)
+            difference(t)
+            weigh(t - 1)
+            turn(t - 1)
+            if t > 1:
+                first_product(t - 2)
+        weigh(PACK - 1)
+        first_product(PACK - 2)
+        half_old = keep.tile([P, 2, 2, HALF], F32, name="half_old", tag="b%d" % (PACK - 1))
+        nc.scalar.activation(half_old[:], old_sb[:].rearrange("p a (h n) -> p h a n", h=2), COPY, scale=0.5)
+        turn(PACK - 1)
+        first_product(PACK - 1)
+
+        w_grouped = [keep.tile([P, HALF, PACK], BF16, name="w_grouped%d" % h, align_bytes=64) for h in range(2)]
+        w_codes = [keep.tile([P, HALF], U32, name="w_codes%d" % h, align_bytes=64) for h in range(2)]
+        w_plane = [keep.tile([P, HALF], U8, name="w_plane%d" % h, align_bytes=64) for h in range(2)]
+        nc.scalar.copy(w_grouped[0][:], w_bank[0][:].rearrange("p t n -> p n t"))
+        nc.vector.tensor_copy(w_grouped[1][:], w_bank[1][:].rearrange("p t n -> p n t"))
+
+        out_rows = out.rearrange("(a p) n -> p a n", p=P)
+        v_bank = [psum.tile([P, 2, HALF], F32, name="v_bank%d" % h) for h in range(2)]
+        for h in range(2):
+            nc.vector.quantize_mx(
+                out=w_codes[h][:].bitcast(E5M2),
+                scales=w_plane[h][:],
+                in_=w_grouped[h][:].rearrange("p n t -> p (n t)"),
+            )
+            for a in range(2):
+                r_cols = slice(a * P, (a + 1) * P)
+                nc.tensor.matmul_mx(
+                    out=v_bank[h][:, a, :],
+                    lhsT=dr_codes[:, r_cols].bitcast(E4M3),
+                    lhsT_scale=dr_plane[:, r_cols],
+                    rhs=w_codes[h][:].bitcast(E5M2),
+                    rhs_scale=w_plane[h][:],
+                    start=True,
+                    stop=True,
+                )
+        for h in range(2):
+            result = keep.tile([P, 2, HALF], F32, name="result%d" % h)
+            nc.vector.scalar_tensor_tensor(result[:], v_bank[h][:], 0.05, half_old[:, h], MULT, ADD)
+            queue = nc.sync if h == 0 else nc.scalar
+            queue.dma_start(out_rows[:, :, h * HALF : (h + 1) * HALF], result[:])

@@ -48,6 +48,11 @@ def tile_list_directions_gaps_stored_mixed_kernel(
         nc.scalar.dma_start(ra_cols[:], ra.rearrange("o (p t) -> (o p) t", t=PACK))
         nc.scalar.dma_start(fk_cols[:], fkr.rearrange("o (p t) -> (o p) t", t=PACK))
 
+        warm_in = keep.tile([P, 1], F32, name="warm_in")
+        warm_out = keep.tile([P, 1], F32, name="warm_out")
+        nc.vector.memset(warm_in[:], 0.0)
+        nc.scalar.activation(warm_out[:], warm_in[:], COPY)
+
         ident = keep.tile([P, P], F32, name="ident")
         make_identity(nc, ident[:])
 

@@ -77,75 +77,84 @@ def tile_list_directions_gaps_stored_mixed_kernel(
             nc.tensor.transpose(ra_all[:, s, :], ra_cols[:, s : s + 1].to_broadcast([P, P]), ident[:])
         ra_by_j = ra_all[:].rearrange("m s q -> m q s")
 
-        b = [keep.tile([P, J], F32, name="b%d" % t, tag="b%d" % t) for t in range(PACK)]
-        d = [keep.tile([P, J], F32, name="d%d" % t) for t in range(PACK)]
+        last = PACK - 1
+        half_j = J // 2
+        b = [keep.tile([P, J], F32, name="b%d" % t, tag="b%d" % t, align_bytes=64) for t in range(PACK)]
         u = [keep.tile([P, J], BF16, name="u%d" % t) for t in range(PACK)]
-        grouped = [keep.tile([P, J], BF16, name="grouped%d" % t, align_bytes=64) for t in range(PACK)]
-        u_codes = [keep.tile([P, P], U32, name="u_codes%d" % t, align_bytes=64) for t in range(PACK)]
-        u_plane = [keep.tile([P, P], U8, name="u_plane%d" % t, align_bytes=64) for t in range(PACK)]
         w_bank = [psum.tile([P, PACK, HALF], F32, name="w_bank%d" % h) for h in range(2)]
+        groups = [(0, 1), (2,), (3,)]
+        turned = [psum.tile([P, len(g), 2, P], F32, name="turned%d" % i, tag="turned%d" % i) for i, g in enumerate(groups)]
+        place = {t: (i, g.index(t)) for i, g in enumerate(groups) for t in g}
 
-        def gather_second(t):
-            nc.scalar.activation(b[t][:], x[t][:].indirect(second[:]), COPY)
+        def picked(t, entries, lo, hi):
+            return x[t][:].indirect(entries[:, lo // PER_COL : hi // PER_COL])
 
-        def difference(t):
-            nc.vector.tensor_tensor(d[t][:], x[t][:].indirect(first[:]), b[t][:], SUB)
-
-        def weigh(t):
-            nc.vector.scalar_tensor_tensor(
-                u[t][:].rearrange("p (q s) -> p q s", s=PACK),
-                d[t][:].rearrange("p (q s) -> p q s", s=PACK),
-                fk_cols[:, t : t + 1],
-                ra_by_j,
-                MULT,
-                MULT,
-            )
-
-        def turn(t):
-            words = u[t][:].bitcast(F32)
-            turned = psum.tile([P, 2, P], F32, name="turned%d" % t, tag="turned%d" % (t % 2))
-            for e in range(2):
-                nc.tensor.transpose(turned[:, e, :], words[:, e::2], ident[:])
-            nc.scalar.copy(
-                grouped[t][:].bitcast(F32).rearrange("p (m e) -> p m e", e=2),
-                turned[:].rearrange("p e m -> p m e"),
-            )
-
-        def first_product(t):
-            nc.vector.quantize_mx(out=u_codes[t][:].bitcast(E4M3), scales=u_plane[t][:], in_=grouped[t][:])
-            for h in range(2):
-                n_cols = slice(h * HALF, (h + 1) * HALF)
-                nc.tensor.matmul_mx(
-                    out=w_bank[h][:, t, :],
-                    lhsT=u_codes[t][:].bitcast(E4M3),
-                    lhsT_scale=u_plane[t][:],
-                    rhs=gj_codes[:, n_cols].bitcast(E5M2),
-                    rhs_scale=gj_plane[:, n_cols],
-                    start=True,
-                    stop=True,
+        def weigh(t, d):
+            for c in range(2):
+                lo, hi = c * half_j, (c + 1) * half_j
+                nc.vector.scalar_tensor_tensor(
+                    u[t][:, lo:hi].rearrange("p (q s) -> p q s", s=PACK),
+                    d[c][:].rearrange("p (q s) -> p q s", s=PACK),
+                    fk_cols[:, t : t + 1],
+                    ra_by_j[:, lo // PACK : hi // PACK, :],
+                    MULT,
+                    MULT,
                 )
+            words = u[t][:].bitcast(F32)
+            i, slot = place[t]
+            for e in range(2):
+                nc.tensor.transpose(turned[i][:, slot, e, :], words[:, e::2], ident[:])
 
-        gather_second(0)
-        difference(0)
-        for t in range(1, PACK):
-            gather_second(t)
-            difference(t)
-            weigh(t - 1)
-            turn(t - 1)
-            if t > 1:
-                first_product(t - 2)
-        weigh(PACK - 1)
-        first_product(PACK - 2)
-        half_old = keep.tile([P, 2, 2, HALF], F32, name="half_old", tag="b%d" % (PACK - 1))
-        nc.scalar.activation(half_old[:], old_sb[:].rearrange("p a (h n) -> p h a n", h=2), COPY, scale=0.5)
-        turn(PACK - 1)
-        first_product(PACK - 1)
+        a_last = keep.tile([P, J], F32, name="a_last")
+        for t in range(PACK):
+            d = [keep.tile([P, half_j], F32, name="d%d_%d" % (t, c), tag="d%d" % c) for c in range(2)]
+            if t == last:
+                nc.scalar.activation(b[t][:], picked(t, second, 0, J), COPY)
+            size = J // 4 if t == 0 else half_j
+            for lo in range(0, J, size):
+                hi = lo + size
+                diff = d[lo // half_j][:, lo % half_j : lo % half_j + size]
+                if t == last:
+                    nc.scalar.activation(a_last[:, lo:hi], picked(t, first, lo, hi), COPY)
+                    nc.vector.tensor_tensor(diff, a_last[:, lo:hi], b[t][:, lo:hi], SUB)
+                else:
+                    nc.scalar.activation(b[t][:, lo:hi], picked(t, second, lo, hi), COPY)
+                    nc.vector.tensor_tensor(diff, picked(t, first, lo, hi), b[t][:, lo:hi], SUB)
+            weigh(t, d)
+
+        for i, g in enumerate(groups):
+            width = len(g) * P
+            tag = "b%d" % (last - 1) if i == 0 else "grouped%d" % i
+            grouped = keep.tile([P, width * PACK], BF16, name="grouped%d" % i, tag=tag, align_bytes=64)
+            u_codes = keep.tile([P, width], U32, name="u_codes%d" % i, tag="u_codes%d" % i, align_bytes=64)
+            u_plane = keep.tile([P, width], U8, name="u_plane%d" % i, align_bytes=64)
+            nc.scalar.copy(
+                grouped[:].bitcast(F32).rearrange("p (a m e) -> p a m e", e=2, m=P),
+                turned[i][:].rearrange("p a e m -> p a m e"),
+            )
+            nc.vector.quantize_mx(out=u_codes[:].bitcast(E4M3), scales=u_plane[:], in_=grouped[:])
+            for slot, t in enumerate(g):
+                k_cols = slice(slot * P, (slot + 1) * P)
+                for h in range(2):
+                    n_cols = slice(h * HALF, (h + 1) * HALF)
+                    nc.tensor.matmul_mx(
+                        out=w_bank[h][:, t, :],
+                        lhsT=u_codes[:, k_cols].bitcast(E4M3),
+                        lhsT_scale=u_plane[:, k_cols],
+                        rhs=gj_codes[:, n_cols].bitcast(E5M2),
+                        rhs_scale=gj_plane[:, n_cols],
+                        start=True,
+                        stop=True,
+                    )
 
         w_grouped = [keep.tile([P, HALF, PACK], BF16, name="w_grouped%d" % h, align_bytes=64) for h in range(2)]
         w_codes = [keep.tile([P, HALF], U32, name="w_codes%d" % h, align_bytes=64) for h in range(2)]
         w_plane = [keep.tile([P, HALF], U8, name="w_plane%d" % h, align_bytes=64) for h in range(2)]
         nc.scalar.copy(w_grouped[0][:], w_bank[0][:].rearrange("p t n -> p n t"))
         nc.vector.tensor_copy(w_grouped[1][:], w_bank[1][:].rearrange("p t n -> p n t"))
+
+        half_old = keep.tile([P, 2, 2, HALF], F32, name="half_old", tag="u_codes%d" % (len(groups) - 1), align_bytes=64)
+        nc.scalar.activation(half_old[:], old_sb[:].rearrange("p a (h n) -> p h a n", h=2), COPY, scale=0.5)
 
         out_rows = out.rearrange("(a p) n -> p a n", p=P)
         v_bank = [psum.tile([P, 2, HALF], F32, name="v_bank%d" % h) for h in range(2)]

@@ -72,7 +72,7 @@ def tile_list_directions_gaps_stored_mixed_kernel(
         nc.sync.dma_start(old_sb[:], old.rearrange("(a p) n -> p a n", p=P))
         dr_codes, dr_plane = load_packed(dr_words, dr_scales, R, "dr")
 
-        ra_all = psum.tile([P, PACK, P], F32, name="ra_all")
+        ra_all = psum.tile([P, PACK, P], F32, name="ra_all", tag="ra_all")
         for s in range(PACK):
             nc.tensor.transpose(ra_all[:, s, :], ra_cols[:, s : s + 1].to_broadcast([P, P]), ident[:])
         ra_by_j = ra_all[:].rearrange("m s q -> m q s")
@@ -89,38 +89,44 @@ def tile_list_directions_gaps_stored_mixed_kernel(
         def picked(t, entries, lo, hi):
             return x[t][:].indirect(entries[:, lo // PER_COL : hi // PER_COL])
 
-        def weigh(t, d):
-            for c in range(2):
-                lo, hi = c * half_j, (c + 1) * half_j
-                nc.vector.scalar_tensor_tensor(
-                    u[t][:, lo:hi].rearrange("p (q s) -> p q s", s=PACK),
-                    d[c][:].rearrange("p (q s) -> p q s", s=PACK),
-                    fk_cols[:, t : t + 1],
-                    ra_by_j[:, lo // PACK : hi // PACK, :],
-                    MULT,
-                    MULT,
-                )
+        plan = [([("sb",0,128),("vb",128,256),("g",0,128),("g",128,256),("sb",256,512),("g",256,384),("sa",384,512),("s",384,512),("u",0,256),("u",256,512)], [0,256,512]), ([("sb",0,256),("g",0,256),("sb",256,512),("g",256,512),("u",0,256),("u",256,512)], [0,256,512]), ([("sb",0,256),("g",0,256),("sb",256,512),("g",256,512),("u",0,256),("u",256,512)], [0,256,512]), ([("sb",0,512),("sa",0,256),("s",0,256),("sa",256,384),("s",256,384),("u",0,256),("sa",384,512),("s",384,512),("u",256,384),("u",384,512)], [0,256,512])]
+
+        a_part = [keep.tile([P, J], F32, name="a_part%d" % t) for t in range(PACK)]
+        for t in range(PACK):
+            steps, cuts = plan[t]
+            d = [
+                keep.tile([P, hi - lo], F32, name="d%d_%d" % (t, c), tag="d%d" % c)
+                for c, (lo, hi) in enumerate(zip(cuts, cuts[1:]))
+            ]
+
+            def diff(lo, hi):
+                c = max(i for i in range(len(d)) if cuts[i] <= lo)
+                return d[c][:, lo - cuts[c] : hi - cuts[c]]
+
+            for kind, lo, hi in steps:
+                if kind == "sb":
+                    nc.scalar.activation(b[t][:, lo:hi], picked(t, second, lo, hi), COPY)
+                elif kind == "vb":
+                    nc.vector.tensor_copy(b[t][:, lo:hi], picked(t, second, lo, hi))
+                elif kind == "sa":
+                    nc.scalar.activation(a_part[t][:, lo:hi], picked(t, first, lo, hi), COPY)
+                elif kind == "g":
+                    nc.vector.tensor_tensor(diff(lo, hi), picked(t, first, lo, hi), b[t][:, lo:hi], SUB)
+                elif kind == "s":
+                    nc.vector.tensor_tensor(diff(lo, hi), a_part[t][:, lo:hi], b[t][:, lo:hi], SUB)
+                else:
+                    nc.vector.scalar_tensor_tensor(
+                        u[t][:, lo:hi].rearrange("p (q s) -> p q s", s=PACK),
+                        diff(lo, hi).rearrange("p (q s) -> p q s", s=PACK),
+                        fk_cols[:, t : t + 1],
+                        ra_by_j[:, lo // PACK : hi // PACK, :],
+                        MULT,
+                        MULT,
+                    )
             words = u[t][:].bitcast(F32)
             i, slot = place[t]
             for e in range(2):
                 nc.tensor.transpose(turned[i][:, slot, e, :], words[:, e::2], ident[:])
-
-        a_last = keep.tile([P, J], F32, name="a_last")
-        for t in range(PACK):
-            d = [keep.tile([P, half_j], F32, name="d%d_%d" % (t, c), tag="d%d" % c) for c in range(2)]
-            if t == last:
-                nc.scalar.activation(b[t][:], picked(t, second, 0, J), COPY)
-            size = J // 4 if t == 0 else half_j
-            for lo in range(0, J, size):
-                hi = lo + size
-                diff = d[lo // half_j][:, lo % half_j : lo % half_j + size]
-                if t == last:
-                    nc.scalar.activation(a_last[:, lo:hi], picked(t, first, lo, hi), COPY)
-                    nc.vector.tensor_tensor(diff, a_last[:, lo:hi], b[t][:, lo:hi], SUB)
-                else:
-                    nc.scalar.activation(b[t][:, lo:hi], picked(t, second, lo, hi), COPY)
-                    nc.vector.tensor_tensor(diff, picked(t, first, lo, hi), b[t][:, lo:hi], SUB)
-            weigh(t, d)
 
         for i, g in enumerate(groups):
             width = len(g) * P
@@ -156,8 +162,8 @@ def tile_list_directions_gaps_stored_mixed_kernel(
         half_old = keep.tile([P, 2, 2, HALF], F32, name="half_old", tag="u_codes%d" % (len(groups) - 1), align_bytes=64)
         nc.scalar.activation(half_old[:], old_sb[:].rearrange("p a (h n) -> p h a n", h=2), COPY, scale=0.5)
 
-        out_rows = out.rearrange("(a p) n -> p a n", p=P)
-        v_bank = [psum.tile([P, 2, HALF], F32, name="v_bank%d" % h) for h in range(2)]
+        free_banks = ["ra_all", "turned0", "turned1", "turned2"]
+        v_bank = {}
         for h in range(2):
             nc.vector.quantize_mx(
                 out=w_codes[h][:].bitcast(E5M2),
@@ -166,8 +172,9 @@ def tile_list_directions_gaps_stored_mixed_kernel(
             )
             for a in range(2):
                 r_cols = slice(a * P, (a + 1) * P)
+                v_bank[h, a] = psum.tile([P, HALF], F32, name="v_bank%d%d" % (h, a), tag=free_banks[2 * h + a])
                 nc.tensor.matmul_mx(
-                    out=v_bank[h][:, a, :],
+                    out=v_bank[h, a][:],
                     lhsT=dr_codes[:, r_cols].bitcast(E4M3),
                     lhsT_scale=dr_plane[:, r_cols],
                     rhs=w_codes[h][:].bitcast(E5M2),
@@ -176,7 +183,8 @@ def tile_list_directions_gaps_stored_mixed_kernel(
                     stop=True,
                 )
         for h in range(2):
-            result = keep.tile([P, 2, HALF], F32, name="result%d" % h)
-            nc.vector.scalar_tensor_tensor(result[:], v_bank[h][:], 0.05, half_old[:, h], MULT, ADD)
-            queue = nc.sync if h == 0 else nc.scalar
-            queue.dma_start(out_rows[:, :, h * HALF : (h + 1) * HALF], result[:])
+            for a in range(2):
+                result = keep.tile([P, HALF], F32, name="result%d%d" % (h, a))
+                nc.vector.scalar_tensor_tensor(result[:], v_bank[h, a][:], 0.05, half_old[:, h, a], MULT, ADD)
+                queue = nc.scalar if a == 0 else nc.sync
+                queue.dma_start(out[a * P : (a + 1) * P, h * HALF : (h + 1) * HALF], result[:])

from contextlib import ExitStack

import concourse.mybir as mybir
from concourse.masks import make_identity

K, J, N, R, T = 512, 512, 256, 256, 1024
FLOPS = 2 * J * K * N + 2 * K * R * N

F32 = mybir.dt.float32
BF16 = mybir.dt.bfloat16
I32 = mybir.dt.int32
U32 = mybir.dt.uint32
U16 = mybir.dt.uint16
U8 = mybir.dt.uint8
E4M3 = mybir.dt.float8_e4m3fn_x4
E5M2 = mybir.dt.float8_e5m2_x4
MULT = mybir.AluOpType.mult
ADD = mybir.AluOpType.add
SUB = mybir.AluOpType.subtract
COPY = mybir.ActivationFunctionType.Copy

P = 128
PACK = 4
PER_COL = 16
HALF = N // 2


def tile_list_directions_gaps_stored_mixed_kernel(
    tc, xf, ra, gj_words, gj_scales, fkr, dr_words, dr_scales, old, offs, offs2, out
):
    nc = tc.nc
    with ExitStack() as ctx:
        keep = ctx.enter_context(tc.tile_pool(name="keep", bufs=1))
        psum = ctx.enter_context(tc.psum_pool(name="psum", bufs=1))

        first = keep.tile([P, J // PER_COL], U16, name="first")
        second = keep.tile([P, J // PER_COL], U16, name="second")
        x_rows = xf.rearrange("(p t) c -> t p c", t=PACK)
        x = [keep.tile([P, T], F32, name="x%d" % t) for t in range(PACK)]
        nc.sync.dma_start(x[0][:], x_rows[0])
        nc.sync.dma_start(second[:], offs2)
        nc.sync.dma_start(first[:], offs)
        for t in range(1, PACK):
            nc.sync.dma_start(x[t][:], x_rows[t])

        ra_cols = keep.tile([P, PACK], F32, name="ra_cols")
        fk_cols = keep.tile([P, PACK], F32, name="fk_cols")
        nc.scalar.dma_start(ra_cols[:], ra.rearrange("o (p t) -> (o p) t", t=PACK))
        nc.scalar.dma_start(fk_cols[:], fkr.rearrange("o (p t) -> (o p) t", t=PACK))

        warm_in = keep.tile([P, 1], F32, name="warm_in")
        warm_out = keep.tile([P, 1], F32, name="warm_out")
        nc.vector.memset(warm_in[:], 0.0)
        nc.scalar.activation(warm_out[:], warm_in[:], COPY)

        ident = keep.tile([P, P], F32, name="ident")
        make_identity(nc, ident[:])

        def load_packed(words, scales, width, name):
            codes = keep.tile([P, width], U32, name=name + "_codes", align_bytes=64)
            plane = keep.tile([P, width], U8, name=name + "_plane", align_bytes=64)
            nc.gpsimd.memset(plane[:].bitcast(I32), 0)
            nc.sync.dma_start(codes[:].bitcast(I32), words[0].rearrange("p n t -> p (n t)").bitcast(I32))
            for q in range(4):
                nc.sync.dma_start(
                    plane[32 * q : 32 * q + 4, :].bitcast(I32), scales[0, 4 * q : 4 * q + 4, :].bitcast(I32)
                )
            return codes, plane

        gj_codes, gj_plane = load_packed(gj_words, gj_scales, N, "gj")
        old_sb = keep.tile([P, 2, N], F32, name="old_sb")
        nc.sync.dma_start(old_sb[:], old.rearrange("(a p) n -> p a n", p=P))
        dr_codes, dr_plane = load_packed(dr_words, dr_scales, R, "dr")

        ra_all = psum.tile([P, PACK, P], F32, name="ra_all", tag="ra_all")
        for s in range(PACK):
            nc.tensor.transpose(ra_all[:, s, :], ra_cols[:, s : s + 1].to_broadcast([P, P]), ident[:])
        ra_by_j = ra_all[:].rearrange("m s q -> m q s")

        last = PACK - 1
        half_j = J // 2
        b = [keep.tile([P, J], F32, name="b%d" % t, tag="b%d" % t, align_bytes=64) for t in range(PACK)]
        u = [keep.tile([P, J], BF16, name="u%d" % t) for t in range(PACK)]
        w_bank = [psum.tile([P, PACK, HALF], F32, name="w_bank%d" % h) for h in range(2)]
        groups = [(0, 1), (2,), (3,)]
        turned = [psum.tile([P, len(g), 2, P], F32, name="turned%d" % i, tag="turned%d" % i) for i, g in enumerate(groups)]
        place = {t: (i, g.index(t)) for i, g in enumerate(groups) for t in g}

        def picked(t, entries, lo, hi):
            return x[t][:].indirect(entries[:, lo // PER_COL : hi // PER_COL])

        plan = [([("sb",0,128),("vb",128,256),("g",0,128),("g",128,256),("sb",256,512),("g",256,384),("sa",384,512),("s",384,512),("u",0,256),("u",256,512)], [0,256,512]), ([("sb",0,256),("g",0,256),("sb",256,512),("g",256,512),("u",0,256),("u",256,512)], [0,256,512]), ([("sb",0,256),("g",0,256),("sb",256,512),("g",256,512),("u",0,256),("u",256,512)], [0,256,512]), ([("sb",0,512),("sa",0,256),("s",0,256),("sa",256,384),("s",256,384),("u",0,256),("sa",384,512),("s",384,512),("u",256,384),("u",384,512)], [0,256,512])]

        a_part = [keep.tile([P, J], F32, name="a_part%d" % t) for t in range(PACK)]
        for t in range(PACK):
            steps, cuts = plan[t]
            d = [
                keep.tile([P, hi - lo], F32, name="d%d_%d" % (t, c), tag="d%d" % c)
                for c, (lo, hi) in enumerate(zip(cuts, cuts[1:]))
            ]

            def diff(lo, hi):
                c = max(i for i in range(len(d)) if cuts[i] <= lo)
                return d[c][:, lo - cuts[c] : hi - cuts[c]]

            for kind, lo, hi in steps:
                if kind == "sb":
                    nc.scalar.activation(b[t][:, lo:hi], picked(t, second, lo, hi), COPY)
                elif kind == "vb":
                    nc.vector.tensor_copy(b[t][:, lo:hi], picked(t, second, lo, hi))
                elif kind == "sa":
                    nc.scalar.activation(a_part[t][:, lo:hi], picked(t, first, lo, hi), COPY)
                elif kind == "g":
                    nc.vector.tensor_tensor(diff(lo, hi), picked(t, first, lo, hi), b[t][:, lo:hi], SUB)
                elif kind == "s":
                    nc.vector.tensor_tensor(diff(lo, hi), a_part[t][:, lo:hi], b[t][:, lo:hi], SUB)
                else:
                    nc.vector.scalar_tensor_tensor(
                        u[t][:, lo:hi].rearrange("p (q s) -> p q s", s=PACK),
                        diff(lo, hi).rearrange("p (q s) -> p q s", s=PACK),
                        fk_cols[:, t : t + 1],
                        ra_by_j[:, lo // PACK : hi // PACK, :],
                        MULT,
                        MULT,
                    )
            words = u[t][:].bitcast(F32)
            i, slot = place[t]
            for e in range(2):
                nc.tensor.transpose(turned[i][:, slot, e, :], words[:, e::2], ident[:])

        for i, g in enumerate(groups):
            width = len(g) * P
            tag = "b%d" % (last - 1) if i == 0 else "grouped%d" % i
            grouped = keep.tile([P, width * PACK], BF16, name="grouped%d" % i, tag=tag, align_bytes=64)
            u_codes = keep.tile([P, width], U32, name="u_codes%d" % i, tag="u_codes%d" % i, align_bytes=64)
            u_plane = keep.tile([P, width], U8, name="u_plane%d" % i, align_bytes=64)
            nc.scalar.copy(
                grouped[:].bitcast(F32).rearrange("p (a m e) -> p a m e", e=2, m=P),
                turned[i][:].rearrange("p a e m -> p a m e"),
            )
            nc.vector.quantize_mx(out=u_codes[:].bitcast(E4M3), scales=u_plane[:], in_=grouped[:])
            for slot, t in enumerate(g):
                k_cols = slice(slot * P, (slot + 1) * P)
                for h in range(2):
                    n_cols = slice(h * HALF, (h + 1) * HALF)
                    nc.tensor.matmul_mx(
                        out=w_bank[h][:, t, :],
                        lhsT=u_codes[:, k_cols].bitcast(E4M3),
                        lhsT_scale=u_plane[:, k_cols],
                        rhs=gj_codes[:, n_cols].bitcast(E5M2),
                        rhs_scale=gj_plane[:, n_cols],
                        start=True,
                        stop=True,
                    )

        w_grouped = [keep.tile([P, HALF, PACK], BF16, name="w_grouped%d" % h, align_bytes=64) for h in range(2)]
        w_codes = [keep.tile([P, HALF], U32, name="w_codes%d" % h, align_bytes=64) for h in range(2)]
        w_plane = [keep.tile([P, HALF], U8, name="w_plane%d" % h, align_bytes=64) for h in range(2)]
        nc.scalar.copy(w_grouped[0][:], w_bank[0][:].rearrange("p t n -> p n t"))
        nc.vector.tensor_copy(w_grouped[1][:], w_bank[1][:].rearrange("p t n -> p n t"))

        half_old = keep.tile([P, 2, 2, HALF], F32, name="half_old", tag="u_codes%d" % (len(groups) - 1), align_bytes=64)
        nc.scalar.activation(half_old[:], old_sb[:].rearrange("p a (h n) -> p h a n", h=2), COPY, scale=0.5)

        free_banks = ["ra_all", "turned0", "turned1", "turned2"]
        v_bank = {}
        for h in range(2):
            nc.vector.quantize_mx(
                out=w_codes[h][:].bitcast(E5M2),
                scales=w_plane[h][:],
                in_=w_grouped[h][:].rearrange("p n t -> p (n t)"),
            )
            for a in range(2):
                r_cols = slice(a * P, (a + 1) * P)
                v_bank[h, a] = psum.tile([P, HALF], F32, name="v_bank%d%d" % (h, a), tag=free_banks[2 * h + a])
                nc.tensor.matmul_mx(
                    out=v_bank[h, a][:],
                    lhsT=dr_codes[:, r_cols].bitcast(E4M3),
                    lhsT_scale=dr_plane[:, r_cols],
                    rhs=w_codes[h][:].bitcast(E5M2),
                    rhs_scale=w_plane[h][:],
                    start=True,
                    stop=True,
                )
        for h in range(2):
            for a in range(2):
                result = keep.tile([P, HALF], F32, name="result%d%d" % (h, a))
                nc.vector.scalar_tensor_tensor(result[:], v_bank[h, a][:], 0.05, half_old[:, h, a], MULT, ADD)
                queue = nc.scalar if a == 0 else nc.sync
                queue.dma_start(out[a * P : (a + 1) * P, h * HALF : (h + 1) * HALF], result[:])
